import numpy as np
import ml_dtypes


def mxq(x, axis, fmt="e4m3"):
    dtype, down = {"e4m3": (ml_dtypes.float8_e4m3fn, 7), "e5m2": (ml_dtypes.float8_e5m2, 14)}[fmt]
    v = np.moveaxis(np.asarray(x, np.float32).astype(ml_dtypes.bfloat16).astype(np.float64), axis, -1)
    blocks = v.reshape(v.shape[:-1] + (-1, 32))
    amax = np.abs(blocks).max(-1, keepdims=True)
    byte = np.maximum(np.where(amax > 0, np.frexp(amax)[1] - 1 + 127, 0) - down, 1)
    scale = np.exp2(byte - 127.0)
    codes = (blocks / scale).astype(np.float32).astype(dtype).astype(np.float64)
    return np.moveaxis((codes * scale).reshape(v.shape), -1, axis)


WIDE = False


def mx_kscale(k):
    if not WIDE:
        return np.ones(k)
    levels = np.array([10, -10, 5, -5, 0])
    if k % 512:
        return np.exp2(np.random.permutation(np.resize(levels, k // 32))).repeat(32)
    a = np.empty((k // 512, 16))
    for p in range(k // 512):
        a[p, :8] = np.random.permutation(np.resize(levels, 8))
        for g in range(8):
            far = levels[np.abs(levels - a[p, g]) >= 10]
            a[p, g + 8] = far[np.random.randint(len(far))]
    return np.exp2(a.ravel()).repeat(32)


def f64(x):
    return np.asarray(x).astype(np.float64)


def striped(idx):
    return np.tile(idx.reshape(-1, 16).T, (8, 1)).astype(np.uint16)


def unstriped(offs):
    return offs[:16].T.reshape(-1).astype(np.int64)


def relu(v):
    return np.maximum(v, 0.0)


K, T, S, V, N = 512, 4096, 1536, 512, 256
P = 2 ** 7


def setup_inputs():
    n = np.random.standard_normal
    s = mx_kscale(K)[:, None]
    return {
        "xT": (n((K, T)) * s).astype(np.float32),
        "w1": (n((K, N)) / np.sqrt(K) / s).astype(np.float32),
        "margin": np.tile(np.random.uniform(0.2, 2.0, V), (P, 1)).astype(np.float32),
        "offs": striped(np.random.permutation(T)[:S]),
    }


def reference(xT, w1, margin, offs):
    xq = mxq(f64(xT)[:, unstriped(offs)], 0, "e4m3")
    h = mxq(f64(w1), 0, "e4m3").T @ xq
    near = (h[:, :V] - h[:, V:2 * V]) ** 2
    far = (h[:, :V] - h[:, 2 * V:3 * V]) ** 2
    return relu(near - far + f64(margin)[:1])

@@ -1,0 +1,124 @@
+from contextlib import ExitStack
+
+import concourse.mybir as mybir
+
+K, T, S, V, M = 512, 4096, 1536, 512, 256
+FLOPS = 2 * K * S * M
+
+F32 = mybir.dt.float32
+BF16 = mybir.dt.bfloat16
+U32 = mybir.dt.uint32
+U16 = mybir.dt.uint16
+U8 = mybir.dt.uint8
+FP8X4 = mybir.dt.float8_e4m3fn_x4
+ACT = mybir.ActivationFunctionType
+ALU = mybir.AluOpType
+
+P = 128
+PACK = 4
+HALF = 256
+
+
+def tile_picked_triplet_none_e_kernel(tc, xT, w1, margin, offs, out):
+    nc = tc.nc
+    with ExitStack() as ctx:
+        keep = ctx.enter_context(tc.tile_pool(name="keep", bufs=1))
+        psum = ctx.enter_context(tc.psum_pool(name="psum", bufs=1))
+
+        offsets = keep.tile([P, S // 16], U16, name="offsets")
+        planes = [keep.tile([P, T], F32, name="plane%d" % j) for j in range(PACK)]
+        w_raw = keep.tile([P, PACK, M], F32, name="w_raw")
+        marg = keep.tile([P, V], F32, name="marg")
+        x_rows = xT.rearrange("(p j) t -> p j t", j=PACK)
+
+        nc.sync.dma_start(planes[0][:], x_rows[:, 0, :])
+        nc.sync.dma_start(offsets[:], offs)
+        nc.sync.dma_start(w_raw[:], w1.rearrange("(p j) m -> p j m", j=PACK))
+        for j in range(1, PACK):
+            nc.sync.dma_start(planes[j][:], x_rows[:, j, :])
+        nc.sync.dma_start(marg[:], margin)
+
+        w_codes, w_scales = [], []
+        w_bf = keep.tile([P, 2, M, PACK], BF16, name="w_bf", align_bytes=64)
+        for s, scale in enumerate((1.0, -1.0)):
+            nc.scalar.activation(w_bf[:, s, :, :], w_raw[:].rearrange("p j m -> p m j"), ACT.Copy, scale=scale)
+        wc = keep.tile([P, 2 * M], U32, name="wc", align_bytes=64)
+        ws = keep.tile([P, 2 * M], U8, name="ws", align_bytes=64)
+
+        picked = [keep.tile([P, V, PACK], BF16, name="picked%d" % q, align_bytes=64) for q in range(3)]
+        codes = [keep.tile([P, V], U32, name="codes%d" % q, align_bytes=64) for q in range(3)]
+        scales = [keep.tile([P, V], U8, name="scales%d" % q, align_bytes=64) for q in range(3)]
+        dense = [keep.tile([P, 2, V], F32, name="dense%d" % q) for q in range(3)]
+
+        def window(j, q):
+            return planes[j][:].indirect(offsets[:, q * (V // 16):(q + 1) * (V // 16)])
+
+        def quantise(q, c0, c1):
+            nc.vector.quantize_mx(out=codes[q][:, c0:c1].bitcast(FP8X4), scales=scales[q][:, c0:c1],
+                                  in_=picked[q][:, c0:c1, :].rearrange("p v j -> p (v j)"))
+
+        for q in range(3):
+            nc.vector.tensor_copy(dense[q][:, 0, :], window(0, q))
+        nc.vector.quantize_mx(out=wc[:].bitcast(FP8X4), scales=ws[:], in_=w_bf[:].rearrange("p s m j -> p (s m j)"))
+        for q in range(3):
+            nc.vector.tensor_copy(dense[q][:, 1, :], window(1, q))
+            nc.scalar.copy(picked[q][:, :, 0:2], dense[q][:].rearrange("p u v -> p v u"))
+        for q in range(3):
+            nc.vector.tensor_copy(picked[q][:, :, 2], window(2, q))
+
+        def mm(bank, h, negated, q, c0, c1, start, stop):
+            m0 = negated * M + h * P
+            nc.tensor.matmul_mx(out=bank, lhsT=wc[:, m0:m0 + P].bitcast(FP8X4), lhsT_scale=ws[:, m0:m0 + P],
+                                rhs=codes[q][:, c0:c1].bitcast(FP8X4), rhs_scale=scales[q][:, c0:c1],
+                                start=start, stop=stop)
+
+        units = [(1, 0), (0, 0), (0, 1), (1, 1)]
+        near_ps = {u: psum.tile([P, HALF], F32, name="near%d%d" % u) for u in units}
+        far_ps = {u: psum.tile([P, HALF], F32, name="far%d%d" % u) for u in units}
+        near = {u: keep.tile([P, HALF], F32, name="nearsb%d%d" % u) for u in units}
+        far = {u: keep.tile([P, HALF], F32, name="farsb%d%d" % u) for u in units}
+        res = {u: keep.tile([P, HALF], F32, name="res%d%d" % u) for u in units}
+        anchor = keep.tile([P, HALF], F32, name="anchor")
+        diff = [keep.tile([P, HALF], F32, name="diff%d" % i) for i in range(2)]
+
+        def cols(u):
+            return u[1] * HALF, (u[1] + 1) * HALF
+
+        nc.vector.tensor_copy(picked[0][:, :, 3], window(3, 0))
+        nc.vector.tensor_copy(picked[1][:, :, 3], window(3, 1))
+        quantise(0, 0, V)
+        quantise(1, 0, V)
+        nc.vector.tensor_copy(picked[2][:, :, 3], window(3, 2))
+
+        plain = units[0]
+        mm(far_ps[plain][:], plain[0], 0, 0, *cols(plain), True, True)
+        nc.scalar.copy(anchor[:], far_ps[plain][:])
+        for u in units[1:]:
+            mm(near_ps[u][:], u[0], 1, 0, *cols(u), True, False)
+        for u in units[1:]:
+            mm(near_ps[u][:], u[0], 0, 1, *cols(u), False, True)
+            nc.scalar.activation(near[u][:], near_ps[u][:], ACT.Square)
+        mm(near_ps[plain][:], plain[0], 0, 1, *cols(plain), True, True)
+        for u in units[1:]:
+            mm(far_ps[u][:], u[0], 1, 0, *cols(u), True, False)
+
+        quantise(2, 0, HALF)
+        quantise(2, HALF, V)
+        nc.vector.tensor_tensor(diff[0][:], near_ps[plain][:], anchor[:], ALU.subtract)
+        nc.scalar.activation(near[plain][:], diff[0][:], ACT.Square)
+        far2 = psum.tile([P, HALF], F32, name="far%d%d" % plain)
+        mm(far2[:], plain[0], 0, 2, *cols(plain), True, True)
+        nc.vector.tensor_tensor(diff[1][:], far2[:], anchor[:], ALU.subtract)
+        nc.scalar.activation(far[plain][:], diff[1][:], ACT.Square)
+        for u in units[1:]:
+            mm(far_ps[u][:], u[0], 0, 2, *cols(u), False, True)
+            nc.scalar.activation(far[u][:], far_ps[u][:], ACT.Square)
+        order = units[1:] + [plain]
+        for u in order:
+            c0, c1 = cols(u)
+            nc.vector.tensor_tensor(near[u][:], near[u][:], marg[:, c0:c1], ALU.add)
+        for u in [units[1], plain, units[2], units[3]]:
+            c0, c1 = cols(u)
+            nc.vector.tensor_tensor(far[u][:], near[u][:], far[u][:], ALU.subtract)
+            nc.vector.tensor_scalar(res[u][:], far[u][:], 0.0, None, ALU.max)
+            nc.sync.dma_start(out[u[0] * P:(u[0] + 1) * P, c0:c1], res[u][:])

@@ -1,6 +1,7 @@
 from contextlib import ExitStack
 
 import concourse.mybir as mybir
+from concourse.masks import make_identity
 
 K, T, S, V, M = 512, 4096, 1536, 512, 256
 FLOPS = 2 * K * S * M
@@ -8,6 +9,7 @@ FLOPS = 2 * K * S * M
 F32 = mybir.dt.float32
 BF16 = mybir.dt.bfloat16
 U32 = mybir.dt.uint32
+I32 = mybir.dt.int32
 U16 = mybir.dt.uint16
 U8 = mybir.dt.uint8
 FP8X4 = mybir.dt.float8_e4m3fn_x4
@@ -17,6 +19,7 @@ ALU = mybir.AluOpType
 P = 128
 PACK = 4
 HALF = 256
+CHUNKS = [[(2048, 2048), (1536, 1024), (512, 352)], [(2048, 1024), (1024, 640), (512, 352), (512, 352)]]
 
 
 def tile_picked_triplet_none_e_kernel(tc, xT, w1, margin, offs, out):
@@ -26,99 +29,164 @@ def tile_picked_triplet_none_e_kernel(tc, xT, w1, margin, offs, out):
         psum = ctx.enter_context(tc.psum_pool(name="psum", bufs=1))
 
         offsets = keep.tile([P, S // 16], U16, name="offsets")
-        planes = [keep.tile([P, T], F32, name="plane%d" % j) for j in range(PACK)]
         w_raw = keep.tile([P, PACK, M], F32, name="w_raw")
-        marg = keep.tile([P, V], F32, name="marg")
+        marg = keep.tile([P, HALF], F32, name="marg")
+        m_rows = keep.tile([P, P], F32, name="m_rows")
         x_rows = xT.rearrange("(p j) t -> p j t", j=PACK)
+        pairs = [keep.tile([P, T, 2], BF16, name="pairs%d" % u, align_bytes=64) for u in range(2)]
 
-        nc.sync.dma_start(planes[0][:], x_rows[:, 0, :])
-        nc.sync.dma_start(offsets[:], offs)
-        nc.sync.dma_start(w_raw[:], w1.rearrange("(p j) m -> p j m", j=PACK))
-        for j in range(1, PACK):
-            nc.sync.dma_start(planes[j][:], x_rows[:, j, :])
-        nc.sync.dma_start(marg[:], margin)
+        raw = {}
+        for u in range(2):
+            c0 = 0
+            for i, (width, share) in enumerate(CHUNKS[u]):
+                raw[(u, i)] = keep.tile([P, 2, width], F32, name="raw%d_%d" % (u, i))
+                nc.sync.dma_start(raw[(u, i)][:], x_rows[:, 2 * u:2 * u + 2, c0:c0 + width])
+                if (u, i) == (0, 0):
+                    nc.sync.dma_start(offsets[:], offs)
+                    nc.sync.dma_start(m_rows[:], margin[0:P // 4, :].rearrange("g (b v) -> (g b) v", v=P))
+                    nc.sync.dma_start(w_raw[:], w1.rearrange("(p j) m -> p j m", j=PACK))
+                c0 = c0 + width
+        nc.sync.dma_start(marg[:], margin[:, 0:HALF])
 
-        w_codes, w_scales = [], []
+        def round_pairs(u):
+            c0 = 0
+            for i, (width, share) in enumerate(CHUNKS[u]):
+                src = raw[(u, i)][:].rearrange("p e t -> p t e")
+                nc.vector.tensor_copy(pairs[u][:, c0:c0 + share, :], src[:, 0:share, :])
+                if share < width:
+                    nc.scalar.copy(pairs[u][:, c0 + share:c0 + width, :], src[:, share:width, :])
+                c0 = c0 + width
+
         w_bf = keep.tile([P, 2, M, PACK], BF16, name="w_bf", align_bytes=64)
         for s, scale in enumerate((1.0, -1.0)):
             nc.scalar.activation(w_bf[:, s, :, :], w_raw[:].rearrange("p j m -> p m j"), ACT.Copy, scale=scale)
         wc = keep.tile([P, 2 * M], U32, name="wc", align_bytes=64)
         ws = keep.tile([P, 2 * M], U8, name="ws", align_bytes=64)
 
-        picked = [keep.tile([P, V, PACK], BF16, name="picked%d" % q, align_bytes=64) for q in range(3)]
+        pieces = [(0, 0, HALF), (0, HALF, V), (1, 0, V), (2, 0, HALF)]
+        picked = {pc: keep.tile([P, pc[2] - pc[1], 2], U32, name="picked%d_%d" % pc[:2], align_bytes=64)[:]
+                  for pc in pieces}
         codes = [keep.tile([P, V], U32, name="codes%d" % q, align_bytes=64) for q in range(3)]
         scales = [keep.tile([P, V], U8, name="scales%d" % q, align_bytes=64) for q in range(3)]
-        dense = [keep.tile([P, 2, V], F32, name="dense%d" % q) for q in range(3)]
+        dense_an = keep.tile([P, 3, V], U32, name="dense_an")
+        dense_p = keep.tile([P, 2, V], U32, name="dense_p", align_bytes=64)
+        picked[(2, HALF, V)] = dense_p[:, 0, :].rearrange("p (v u) -> p v u", u=2)
+        dense = [dense_an[:, 1:3, :], dense_p[:], dense_an[:, 0:3:2, :]]
 
-        def window(j, q):
-            return planes[j][:].indirect(offsets[:, q * (V // 16):(q + 1) * (V // 16)])
+        def gather(u, q):
+            words = pairs[u][:].rearrange("p t e -> p (t e)").bitcast(U32)
+            nc.vector.tensor_copy(dense[q][:, u, :], words.indirect(offsets[:, q * (V // 16):(q + 1) * (V // 16)]))
+
+        def weave(q, c0, c1):
+            src = dense[q][:, :, c0:c1]
+            if (q, c0) in [(2, HALF)]:
+                nc.vector.tensor_copy(picked[(q, c0, c1)].bitcast(I32), src.bitcast(I32).rearrange("p u v -> p v u"))
+            else:
+                nc.scalar.copy(picked[(q, c0, c1)], src.rearrange("p u v -> p v u"))
 
         def quantise(q, c0, c1):
             nc.vector.quantize_mx(out=codes[q][:, c0:c1].bitcast(FP8X4), scales=scales[q][:, c0:c1],
-                                  in_=picked[q][:, c0:c1, :].rearrange("p v j -> p (v j)"))
+                                  in_=picked[(q, c0, c1)].rearrange("p v u -> p (v u)").bitcast(BF16))
 
-        for q in range(3):
-            nc.vector.tensor_copy(dense[q][:, 0, :], window(0, q))
+        round_pairs(0)
         nc.vector.quantize_mx(out=wc[:].bitcast(FP8X4), scales=ws[:], in_=w_bf[:].rearrange("p s m j -> p (s m j)"))
         for q in range(3):
-            nc.vector.tensor_copy(dense[q][:, 1, :], window(1, q))
-            nc.scalar.copy(picked[q][:, :, 0:2], dense[q][:].rearrange("p u v -> p v u"))
-        for q in range(3):
-            nc.vector.tensor_copy(picked[q][:, :, 2], window(2, q))
+            gather(0, q)
+        round_pairs(1)
 
-        def mm(bank, h, negated, q, c0, c1, start, stop):
-            m0 = negated * M + h * P
-            nc.tensor.matmul_mx(out=bank, lhsT=wc[:, m0:m0 + P].bitcast(FP8X4), lhsT_scale=ws[:, m0:m0 + P],
-                                rhs=codes[q][:, c0:c1].bitcast(FP8X4), rhs_scale=scales[q][:, c0:c1],
-                                start=start, stop=stop)
+        ident = keep.tile([P, P], F32, name="ident")
+        make_identity(nc, ident[:])
 
-        units = [(1, 0), (0, 0), (0, 1), (1, 1)]
-        near_ps = {u: psum.tile([P, HALF], F32, name="near%d%d" % u) for u in units}
+        def turn(dst, src, start, stop):
+            nc.tensor.matmul(dst, src, ident[:], start=start, stop=stop, is_transpose=True)
+
+        m_ps = psum.tile([P, P], F32, name="bank_turned")
+        turn(m_ps[:], m_rows[:], True, True)
+        m_col = keep.tile([P, 4], F32, name="m_col")
+        nc.scalar.copy(m_col[:], m_ps[:, 0:4])
+        sum_ps = psum.tile([P, 2, 2, P], F32, name="bank_sum")
+        for h in range(2):
+            for b in range(2):
+                turn(sum_ps[:, h, b, :], m_col[:, 2 + b:3 + b].to_broadcast([P, P]), h + b == 0, False)
+
+        def weights(negated, m0, m1):
+            return wc[:, negated * M + m0:negated * M + m1].bitcast(FP8X4), ws[:, negated * M + m0:negated * M + m1]
+
+        def half_w(negated, h):
+            return weights(negated, h * P, (h + 1) * P)
+
+        def samples(q, c0, c1):
+            return codes[q][:, c0:c1].bitcast(FP8X4), scales[q][:, c0:c1]
+
+        def mm(dst, stationary, moving, start, stop):
+            nc.tensor.matmul_mx(out=dst, lhsT=stationary[0], lhsT_scale=stationary[1],
+                                rhs=moving[0], rhs_scale=moving[1], start=start, stop=stop)
+
+        units = [(0, 0), (1, 0), (0, 1), (1, 1)]
+        plain = (1, 0)
+        folded = [u for u in units if u != plain]
+        near_ps = {u: psum.tile([P, HALF], F32, name="near%d%d" % u) for u in units[:2]}
+        turned_ps = psum.tile([P, 2, M], F32, name="bank_turned")
         far_ps = {u: psum.tile([P, HALF], F32, name="far%d%d" % u) for u in units}
-        near = {u: keep.tile([P, HALF], F32, name="nearsb%d%d" % u) for u in units}
+        near = {u: keep.tile([P, HALF], F32, name="nearsb%d%d" % u) for u in units[:2]}
+        turned = keep.tile([P, 2, M], F32, name="turned")
         far = {u: keep.tile([P, HALF], F32, name="farsb%d%d" % u) for u in units}
         res = {u: keep.tile([P, HALF], F32, name="res%d%d" % u) for u in units}
         anchor = keep.tile([P, HALF], F32, name="anchor")
-        diff = [keep.tile([P, HALF], F32, name="diff%d" % i) for i in range(2)]
+        diff = [dense_an[:, 0, 0:HALF].bitcast(F32), dense_an[:, 2, 0:HALF].bitcast(F32)]
 
         def cols(u):
             return u[1] * HALF, (u[1] + 1) * HALF
 
-        nc.vector.tensor_copy(picked[0][:, :, 3], window(3, 0))
-        nc.vector.tensor_copy(picked[1][:, :, 3], window(3, 1))
-        quantise(0, 0, V)
+        gather(1, 0)
+        weave(0, 0, HALF)
+        weave(0, HALF, V)
+        gather(1, 1)
+        weave(1, 0, V)
+        quantise(0, 0, HALF)
+        quantise(0, HALF, V)
+        gather(1, 2)
         quantise(1, 0, V)
-        nc.vector.tensor_copy(picked[2][:, :, 3], window(3, 2))
 
-        plain = units[0]
-        mm(far_ps[plain][:], plain[0], 0, 0, *cols(plain), True, True)
+        mm(far_ps[plain][:], half_w(0, plain[0]), samples(0, *cols(plain)), True, True)
         nc.scalar.copy(anchor[:], far_ps[plain][:])
-        for u in units[1:]:
-            mm(near_ps[u][:], u[0], 1, 0, *cols(u), True, False)
-        for u in units[1:]:
-            mm(near_ps[u][:], u[0], 0, 1, *cols(u), False, True)
-            nc.scalar.activation(near[u][:], near_ps[u][:], ACT.Square)
-        mm(near_ps[plain][:], plain[0], 0, 1, *cols(plain), True, True)
-        for u in units[1:]:
-            mm(far_ps[u][:], u[0], 1, 0, *cols(u), True, False)
-
+        weave(2, 0, HALF)
+        weave(2, HALF, V)
         quantise(2, 0, HALF)
         quantise(2, HALF, V)
-        nc.vector.tensor_tensor(diff[0][:], near_ps[plain][:], anchor[:], ALU.subtract)
-        nc.scalar.activation(near[plain][:], diff[0][:], ACT.Square)
-        far2 = psum.tile([P, HALF], F32, name="far%d%d" % plain)
-        mm(far2[:], plain[0], 0, 2, *cols(plain), True, True)
-        nc.vector.tensor_tensor(diff[1][:], far2[:], anchor[:], ALU.subtract)
-        nc.scalar.activation(far[plain][:], diff[1][:], ACT.Square)
-        for u in units[1:]:
-            mm(far_ps[u][:], u[0], 0, 2, *cols(u), False, True)
-            nc.scalar.activation(far[u][:], far_ps[u][:], ACT.Square)
-        order = units[1:] + [plain]
-        for u in order:
+        mm(near_ps[(0, 0)][:], half_w(1, 0), samples(0, 0, HALF), True, False)
+        mm(far_ps[(0, 0)][:], half_w(1, 0), samples(0, 0, HALF), True, False)
+        for b in range(2):
+            mm(turned_ps[:, b, :], samples(0, HALF + b * P, HALF + (b + 1) * P), weights(1, 0, M), b == 0, False)
+        for u in units[2:]:
+            mm(far_ps[u][:], half_w(1, u[0]), samples(0, *cols(u)), True, False)
+        for u in [plain, (0, 0)]:
+            mm(near_ps[u][:], half_w(0, u[0]), samples(1, *cols(u)), u == plain, True)
+        for b in range(2):
+            mm(turned_ps[:, b, :], samples(1, HALF + b * P, HALF + (b + 1) * P), weights(0, 0, M), False, b == 1)
+        far_ps[plain] = psum.tile([P, HALF], F32, name="far%d%d" % plain)
+        for u in [plain] + folded:
+            mm(far_ps[u][:], half_w(0, u[0]), samples(2, *cols(u)), u == plain, True)
+
+        first = units[0]
+        nc.vector.tensor_tensor(diff[0], near_ps[plain][:], anchor[:], ALU.subtract)
+        nc.scalar.activation(near[first][:], near_ps[first][:], ACT.Square)
+        nc.vector.tensor_tensor(near[first][:], near[first][:], marg[:], ALU.add)
+        nc.scalar.activation(turned[:], turned_ps[:], ACT.Square)
+        for h in range(2):
+            for b in range(2):
+                turn(sum_ps[:, h, b, :], turned[:, b, h * P:(h + 1) * P], False, h + b == 2)
+        nc.vector.tensor_tensor(diff[1], far_ps[plain][:], anchor[:], ALU.subtract)
+        nc.scalar.activation(near[plain][:], diff[0], ACT.Square)
+        nc.vector.tensor_tensor(near[plain][:], near[plain][:], marg[:], ALU.add)
+        for u in units:
+            nc.scalar.activation(far[u][:], diff[1] if u == plain else far_ps[u][:], ACT.Square)
+            lhs = near[u][:] if u[1] == 0 else sum_ps[:, u[0], :, :].rearrange("p b v -> p (b v)")
+            nc.vector.tensor_tensor(far[u][:], lhs, far[u][:], ALU.subtract)
+        for u in units:
             c0, c1 = cols(u)
-            nc.vector.tensor_tensor(near[u][:], near[u][:], marg[:, c0:c1], ALU.add)
-        for u in [units[1], plain, units[2], units[3]]:
-            c0, c1 = cols(u)
-            nc.vector.tensor_tensor(far[u][:], near[u][:], far[u][:], ALU.subtract)
-            nc.vector.tensor_scalar(res[u][:], far[u][:], 0.0, None, ALU.max)
+            if u in [(1, 1)]:
+                nc.vector.tensor_scalar(res[u][:], far[u][:], 0.0, None, ALU.max)
+            else:
+                nc.scalar.activation(res[u][:], far[u][:], ACT.Relu)
             nc.sync.dma_start(out[u[0] * P:(u[0] + 1) * P, c0:c1], res[u][:])

from contextlib import ExitStack

import concourse.mybir as mybir
from concourse.masks import make_identity

K, T, S, V, M = 512, 4096, 1536, 512, 256
FLOPS = 2 * K * S * M

F32 = mybir.dt.float32
BF16 = mybir.dt.bfloat16
U32 = mybir.dt.uint32
I32 = mybir.dt.int32
U16 = mybir.dt.uint16
U8 = mybir.dt.uint8
FP8X4 = mybir.dt.float8_e4m3fn_x4
ACT = mybir.ActivationFunctionType
ALU = mybir.AluOpType

P = 128
PACK = 4
HALF = 256
CHUNKS = [[(2048, 2048), (1536, 1024), (512, 352)], [(2048, 1024), (1024, 640), (512, 352), (512, 352)]]


def tile_picked_triplet_none_e_kernel(tc, xT, w1, margin, offs, out):
    nc = tc.nc
    with ExitStack() as ctx:
        keep = ctx.enter_context(tc.tile_pool(name="keep", bufs=1))
        psum = ctx.enter_context(tc.psum_pool(name="psum", bufs=1))

        offsets = keep.tile([P, S // 16], U16, name="offsets")
        w_raw = keep.tile([P, PACK, M], F32, name="w_raw")
        marg = keep.tile([P, HALF], F32, name="marg")
        m_rows = keep.tile([P, P], F32, name="m_rows")
        x_rows = xT.rearrange("(p j) t -> p j t", j=PACK)
        pairs = [keep.tile([P, T, 2], BF16, name="pairs%d" % u, align_bytes=64) for u in range(2)]

        raw = {}
        for u in range(2):
            c0 = 0
            for i, (width, share) in enumerate(CHUNKS[u]):
                raw[(u, i)] = keep.tile([P, 2, width], F32, name="raw%d_%d" % (u, i))
                nc.sync.dma_start(raw[(u, i)][:], x_rows[:, 2 * u:2 * u + 2, c0:c0 + width])
                if (u, i) == (0, 0):
                    nc.sync.dma_start(offsets[:], offs)
                    nc.sync.dma_start(m_rows[:], margin[0:P // 4, :].rearrange("g (b v) -> (g b) v", v=P))
                    nc.sync.dma_start(w_raw[:], w1.rearrange("(p j) m -> p j m", j=PACK))
                c0 = c0 + width
        nc.sync.dma_start(marg[:], margin[:, 0:HALF])

        def round_pairs(u):
            c0 = 0
            for i, (width, share) in enumerate(CHUNKS[u]):
                src = raw[(u, i)][:].rearrange("p e t -> p t e")
                nc.vector.tensor_copy(pairs[u][:, c0:c0 + share, :], src[:, 0:share, :])
                if share < width:
                    nc.scalar.copy(pairs[u][:, c0 + share:c0 + width, :], src[:, share:width, :])
                c0 = c0 + width

        w_bf = keep.tile([P, 2, M, PACK], BF16, name="w_bf", align_bytes=64)
        for s, scale in enumerate((1.0, -1.0)):
            nc.scalar.activation(w_bf[:, s, :, :], w_raw[:].rearrange("p j m -> p m j"), ACT.Copy, scale=scale)
        wc = keep.tile([P, 2 * M], U32, name="wc", align_bytes=64)
        ws = keep.tile([P, 2 * M], U8, name="ws", align_bytes=64)

        pieces = [(0, 0, HALF), (0, HALF, V), (1, 0, V), (2, 0, HALF)]
        picked = {pc: keep.tile([P, pc[2] - pc[1], 2], U32, name="picked%d_%d" % pc[:2], align_bytes=64)[:]
                  for pc in pieces}
        codes = [keep.tile([P, V], U32, name="codes%d" % q, align_bytes=64) for q in range(3)]
        scales = [keep.tile([P, V], U8, name="scales%d" % q, align_bytes=64) for q in range(3)]
        dense_an = keep.tile([P, 3, V], U32, name="dense_an")
        dense_p = keep.tile([P, 2, V], U32, name="dense_p", align_bytes=64)
        picked[(2, HALF, V)] = dense_p[:, 0, :].rearrange("p (v u) -> p v u", u=2)
        dense = [dense_an[:, 1:3, :], dense_p[:], dense_an[:, 0:3:2, :]]

        def gather(u, q):
            words = pairs[u][:].rearrange("p t e -> p (t e)").bitcast(U32)
            nc.vector.tensor_copy(dense[q][:, u, :], words.indirect(offsets[:, q * (V // 16):(q + 1) * (V // 16)]))

        def weave(q, c0, c1):
            src = dense[q][:, :, c0:c1]
            if (q, c0) in [(2, HALF)]:
                nc.vector.tensor_copy(picked[(q, c0, c1)].bitcast(I32), src.bitcast(I32).rearrange("p u v -> p v u"))
            else:
                nc.scalar.copy(picked[(q, c0, c1)], src.rearrange("p u v -> p v u"))

        def quantise(q, c0, c1):
            nc.vector.quantize_mx(out=codes[q][:, c0:c1].bitcast(FP8X4), scales=scales[q][:, c0:c1],
                                  in_=picked[(q, c0, c1)].rearrange("p v u -> p (v u)").bitcast(BF16))

        round_pairs(0)
        nc.vector.quantize_mx(out=wc[:].bitcast(FP8X4), scales=ws[:], in_=w_bf[:].rearrange("p s m j -> p (s m j)"))
        for q in range(3):
            gather(0, q)
        round_pairs(1)

        ident = keep.tile([P, P], F32, name="ident")
        make_identity(nc, ident[:])

        def turn(dst, src, start, stop):
            nc.tensor.matmul(dst, src, ident[:], start=start, stop=stop, is_transpose=True)

        m_ps = psum.tile([P, P], F32, name="bank_turned")
        turn(m_ps[:], m_rows[:], True, True)
        m_col = keep.tile([P, 4], F32, name="m_col")
        nc.scalar.copy(m_col[:], m_ps[:, 0:4])
        sum_ps = psum.tile([P, 2, 2, P], F32, name="bank_sum")
        for h in range(2):
            for b in range(2):
                turn(sum_ps[:, h, b, :], m_col[:, 2 + b:3 + b].to_broadcast([P, P]), h + b == 0, False)

        def weights(negated, m0, m1):
            return wc[:, negated * M + m0:negated * M + m1].bitcast(FP8X4), ws[:, negated * M + m0:negated * M + m1]

        def half_w(negated, h):
            return weights(negated, h * P, (h + 1) * P)

        def samples(q, c0, c1):
            return codes[q][:, c0:c1].bitcast(FP8X4), scales[q][:, c0:c1]

        def mm(dst, stationary, moving, start, stop):
            nc.tensor.matmul_mx(out=dst, lhsT=stationary[0], lhsT_scale=stationary[1],
                                rhs=moving[0], rhs_scale=moving[1], start=start, stop=stop)

        units = [(0, 0), (1, 0), (0, 1), (1, 1)]
        plain = (1, 0)
        folded = [u for u in units if u != plain]
        near_ps = {u: psum.tile([P, HALF], F32, name="near%d%d" % u) for u in units[:2]}
        turned_ps = psum.tile([P, 2, M], F32, name="bank_turned")
        far_ps = {u: psum.tile([P, HALF], F32, name="far%d%d" % u) for u in units}
        near = {u: keep.tile([P, HALF], F32, name="nearsb%d%d" % u) for u in units[:2]}
        turned = keep.tile([P, 2, M], F32, name="turned")
        far = {u: keep.tile([P, HALF], F32, name="farsb%d%d" % u) for u in units}
        res = {u: keep.tile([P, HALF], F32, name="res%d%d" % u) for u in units}
        anchor = keep.tile([P, HALF], F32, name="anchor")
        diff = [dense_an[:, 0, 0:HALF].bitcast(F32), dense_an[:, 2, 0:HALF].bitcast(F32)]

        def cols(u):
            return u[1] * HALF, (u[1] + 1) * HALF

        gather(1, 0)
        weave(0, 0, HALF)
        weave(0, HALF, V)
        gather(1, 1)
        weave(1, 0, V)
        quantise(0, 0, HALF)
        quantise(0, HALF, V)
        gather(1, 2)
        quantise(1, 0, V)

        mm(far_ps[plain][:], half_w(0, plain[0]), samples(0, *cols(plain)), True, True)
        nc.scalar.copy(anchor[:], far_ps[plain][:])
        weave(2, 0, HALF)
        weave(2, HALF, V)
        quantise(2, 0, HALF)
        quantise(2, HALF, V)
        mm(near_ps[(0, 0)][:], half_w(1, 0), samples(0, 0, HALF), True, False)
        mm(far_ps[(0, 0)][:], half_w(1, 0), samples(0, 0, HALF), True, False)
        for b in range(2):
            mm(turned_ps[:, b, :], samples(0, HALF + b * P, HALF + (b + 1) * P), weights(1, 0, M), b == 0, False)
        for u in units[2:]:
            mm(far_ps[u][:], half_w(1, u[0]), samples(0, *cols(u)), True, False)
        for u in [plain, (0, 0)]:
            mm(near_ps[u][:], half_w(0, u[0]), samples(1, *cols(u)), u == plain, True)
        for b in range(2):
            mm(turned_ps[:, b, :], samples(1, HALF + b * P, HALF + (b + 1) * P), weights(0, 0, M), False, b == 1)
        far_ps[plain] = psum.tile([P, HALF], F32, name="far%d%d" % plain)
        for u in [plain] + folded:
            mm(far_ps[u][:], half_w(0, u[0]), samples(2, *cols(u)), u == plain, True)

        first = units[0]
        nc.vector.tensor_tensor(diff[0], near_ps[plain][:], anchor[:], ALU.subtract)
        nc.scalar.activation(near[first][:], near_ps[first][:], ACT.Square)
        nc.vector.tensor_tensor(near[first][:], near[first][:], marg[:], ALU.add)
        nc.scalar.activation(turned[:], turned_ps[:], ACT.Square)
        for h in range(2):
            for b in range(2):
                turn(sum_ps[:, h, b, :], turned[:, b, h * P:(h + 1) * P], False, h + b == 2)
        nc.vector.tensor_tensor(diff[1], far_ps[plain][:], anchor[:], ALU.subtract)
        nc.scalar.activation(near[plain][:], diff[0], ACT.Square)
        nc.vector.tensor_tensor(near[plain][:], near[plain][:], marg[:], ALU.add)
        for u in units:
            nc.scalar.activation(far[u][:], diff[1] if u == plain else far_ps[u][:], ACT.Square)
            lhs = near[u][:] if u[1] == 0 else sum_ps[:, u[0], :, :].rearrange("p b v -> p (b v)")
            nc.vector.tensor_tensor(far[u][:], lhs, far[u][:], ALU.subtract)
        for u in units:
            c0, c1 = cols(u)
            if u in [(1, 1)]:
                nc.vector.tensor_scalar(res[u][:], far[u][:], 0.0, None, ALU.max)
            else:
                nc.scalar.activation(res[u][:], far[u][:], ACT.Relu)
            nc.sync.dma_start(out[u[0] * P:(u[0] + 1) * P, c0:c1], res[u][:])
